import numpy as np
import ml_dtypes


def mxq(x, axis, fmt="e4m3"):
    dtype, down = {"e4m3": (ml_dtypes.float8_e4m3fn, 7), "e5m2": (ml_dtypes.float8_e5m2, 14)}[fmt]
    v = np.moveaxis(np.asarray(x, np.float32).astype(ml_dtypes.bfloat16).astype(np.float64), axis, -1)
    blocks = v.reshape(v.shape[:-1] + (-1, 32))
    amax = np.abs(blocks).max(-1, keepdims=True)
    byte = np.maximum(np.where(amax > 0, np.frexp(amax)[1] - 1 + 127, 0) - down, 1)
    scale = np.exp2(byte - 127.0)
    codes = (blocks / scale).astype(np.float32).astype(dtype).astype(np.float64)
    return np.moveaxis((codes * scale).reshape(v.shape), -1, axis)


WIDE = False


def mx_kscale(k):
    if not WIDE:
        return np.ones(k)
    levels = np.array([30, -30])
    if k % 512:
        return np.exp2(np.random.permutation(np.resize(levels, k // 32))).repeat(32)
    a = np.empty((k // 512, 16))
    for p in range(k // 512):
        a[p, :8] = np.random.permutation(np.resize(levels, 8))
        for g in range(8):
            far = levels[np.abs(levels - a[p, g]) >= 10]
            a[p, g + 8] = far[np.random.randint(len(far))]
    return np.exp2(a.ravel()).repeat(32)


BF16 = ml_dtypes.bfloat16


def bf(x):
    return np.asarray(x, np.float32).astype(BF16)


def f64(x):
    return np.asarray(x).astype(np.float64)


E2M1 = np.array([0.0, 0.5, 1.0, 1.5, 2.0, 3.0, 4.0, 6.0, -0.0, -0.5, -1.0, -1.5, -2.0, -3.0, -4.0, -6.0])


def pack_weight(w, fmt):
    k, n = w.shape
    w = f64(bf(w)).reshape(k // 32, 32, n)
    amax = np.abs(w).max(1)
    if fmt in ("e4m3", "e5m2"):
        byte = np.frexp(amax)[1] - 1 + 127 - (7 if fmt == "e4m3" else 14)
    else:
        mant, ex = np.frexp(amax / 6.0)
        byte = np.where(mant > 0.5, ex, ex - 1) + 127
    byte = np.clip(np.where(amax > 0, byte, 1), 1, 254)
    scaled = (w * np.exp2(127.0 - byte)[:, None, :]).reshape(k, n).astype(np.float32)
    by_word = np.ascontiguousarray(scaled.reshape(k // 512, 128, 4, n).transpose(0, 1, 3, 2))
    if fmt in ("e4m3", "e5m2"):
        words = by_word.astype(ml_dtypes.float8_e4m3fn if fmt == "e4m3" else ml_dtypes.float8_e5m2).view(np.uint8)
    else:
        c = by_word.astype(ml_dtypes.float4_e2m1fn).view(np.uint8) & 0xF
        words = c[..., 0::2] | (c[..., 1::2] << 4)
    return np.ascontiguousarray(words), np.ascontiguousarray(byte.astype(np.uint8).reshape(k // 512, 16, n))


def unpack_weight(words, scales, fmt):
    g, p, n, _ = words.shape
    if fmt in ("e4m3", "e5m2"):
        vals = np.ascontiguousarray(words).view(ml_dtypes.float8_e4m3fn if fmt == "e4m3" else ml_dtypes.float8_e5m2).astype(np.float64)
    else:
        nib = np.empty((g, p, n, 4), np.uint8)
        nib[..., 0::2] = words & 0xF
        nib[..., 1::2] = words >> 4
        vals = E2M1[nib]
    vals = vals * np.repeat(np.exp2(scales.astype(np.float64) - 127.0), 8, axis=1)[..., None]
    return vals.transpose(0, 1, 3, 2).reshape(g * 512, n)


T, K, P = 512, 4096, 1536


def setup_inputs():
    s = mx_kscale(K)
    G = np.random.standard_normal((K, T)) * np.exp(0.7 * np.random.standard_normal((K, T))) * s[:, None]
    g_words, g_scales = pack_weight(G, "e5m2")
    return {"g_words": g_words,
            "g_scales": g_scales,
            "mixed": bf(np.random.standard_normal((P, K)) / np.sqrt(K) / s),
            "direct": bf(0.5 * np.random.standard_normal((T, P))),
            "eta": bf(0.5 * np.exp(0.3 * np.random.standard_normal(T))),
            "rho": bf(0.3 * np.random.standard_normal(P))}


def reference(g_words, g_scales, mixed, direct, eta, rho):
    G = unpack_weight(g_words, g_scales, "e5m2")
    mq = mxq(f64(mixed), 1, "e4m3")
    through = G.T @ mq.T
    dlam = f64(direct) - f64(eta)[:, None] * through
    return dlam * np.exp(f64(rho))

@@ -1,0 +1,259 @@
+from contextlib import ExitStack
+
+import concourse.mybir as mybir
+from concourse.masks import make_identity
+
+T, K, J = 512, 4096, 1536
+FLOPS = 2 * T * K * J
+
+F32 = mybir.dt.float32
+BF16 = mybir.dt.bfloat16
+I32 = mybir.dt.int32
+U32 = mybir.dt.uint32
+U8 = mybir.dt.uint8
+E4X4 = mybir.dt.float8_e4m3fn_x4
+E5X4 = mybir.dt.float8_e5m2_x4
+EXP = mybir.ActivationFunctionType.Exp
+MULT = mybir.AluOpType.mult
+ADD = mybir.AluOpType.add
+
+N = 512
+SWEEPS = J // N
+PAIRS = K // 1024
+NP = SWEEPS * PAIRS
+
+
+def tile_multitask_unrolled_hypergradient_e1_kernel(
+    tc, g_words, g_scales, mixed, direct, eta, rho, out
+):
+    nc = tc.nc
+    with ExitStack() as ctx:
+        keep = ctx.enter_context(tc.tile_pool(name="keep", bufs=1))
+        work = ctx.enter_context(tc.tile_pool(name="work", bufs=4))
+        psum = ctx.enter_context(tc.psum_pool(name="psum", bufs=1))
+        ctx.enter_context(tc.manual_schedule())
+
+        gw = keep.tile([128, 8, T], U32, name="gw", align_bytes=64)
+        gs = keep.tile([128, 8, T], U8, name="gs", align_bytes=64)
+        vec = keep.tile([128, 128], BF16, name="vec", align_bytes=64)
+        vect = keep.tile([128, 16], BF16, name="vect", align_bytes=64)
+        neg_eta = keep.tile([128, 4], F32, name="neg_eta")
+        e_all = keep.tile([128, J], F32, name="e_all", align_bytes=64)
+        ident = keep.tile([128, 128], F32, name="ident", align_bytes=64)
+        ident_bf = keep.tile([128, 128], BF16, name="ident_bf", align_bytes=64)
+
+        raws = {}
+        dirs = {}
+
+        def load_m(h, pieces):
+            s, q = divmod(h, PAIRS)
+            raw = work.tile([128, 4, 1024], BF16, name="raw", tag="raw", bufs=12, align_bytes=64)
+            raws[h] = raw
+            src = mixed[s * N : (s + 1) * N, q * 1024 : (q + 1) * 1024].rearrange("(r p) k -> p r k", p=128)
+            for rs, ks in pieces:
+                nc.sync.dma_start(out=raw[:, rs, ks], in_=src[:, rs, ks])
+
+        def load_g(q):
+            src = g_words.rearrange("g p n t -> g p (n t)").bitcast(I32)
+            nc.sync.dma_start(
+                out=gw[:, 2 * q : 2 * q + 2, :].bitcast(I32),
+                in_=src[2 * q : 2 * q + 2].rearrange("g p n -> p g n"),
+            )
+
+        def load_d(s):
+            d = keep.tile([128, 4, N], BF16, name="d%d" % s, align_bytes=64)
+            dirs[s] = d
+            nc.sync.dma_start(out=d[:], in_=direct[:, s * N : (s + 1) * N].rearrange("(m p) j -> p m j", p=128))
+
+        WHOLE = [(slice(0, 4), slice(0, 1024))]
+        nc.vector.memset(vec[:], 0.0)
+        nc.scalar.dma_start(out=vec[0:12, :], in_=rho.rearrange("(c p) -> c p", p=128))
+        nc.scalar.dma_start(out=vec[12:16, :], in_=eta.rearrange("(c p) -> c p", p=128))
+        make_identity(nc, ident_bf[:])
+        make_identity(nc, ident[:])
+        nc.vector.memset(gs[:].bitcast(I32), 0)
+        load_m(0, [(slice(2 * b, 2 * b + 2), slice(512 * g, 512 * g + 512)) for g in range(2) for b in range(2)])
+        for Q in range(4):
+            nc.sync.dma_start(
+                out=gs[32 * Q : 32 * Q + 4].bitcast(I32),
+                in_=g_scales[:, 4 * Q : 4 * Q + 4, :].bitcast(I32).rearrange("g r n -> r g n"),
+            )
+        load_g(0)
+        load_m(1, WHOLE)
+        load_m(2, WHOLE)
+        load_g(1)
+        load_m(3, WHOLE)
+        load_g(2)
+        load_m(4, WHOLE)
+        load_g(3)
+        load_d(0)
+        load_m(5, WHOLE)
+        load_m(6, WHOLE)
+        load_d(1)
+        load_m(7, WHOLE)
+        load_m(8, WHOLE)
+        load_m(9, WHOLE)
+        load_d(2)
+
+        acc = {}
+
+        def new_acc(m, shape, dtype):
+            return psum.tile(shape, dtype, name="acc%d" % m, tag="acc%d" % m, bufs=1)
+
+        vps = new_acc(2, [128, 128], BF16)
+        nc.tensor.transpose(vps[:], vec[:], ident_bf[:])
+        nc.vector.tensor_copy(out=vect[:], in_=vps[:, 0:16])
+        nc.vector.tensor_scalar(out=neg_eta[:], in0=vect[:, 12:16], scalar1=-1.0, scalar2=None, op0=MULT)
+        eb = [new_acc(0, [128, 1024], BF16), new_acc(1, [128, 512], BF16)]
+        for c in range(12):
+            nc.tensor.transpose(
+                eb[c // 8][:, (c % 8) * 128 : (c % 8 + 1) * 128],
+                vect[:, c : c + 1].to_broadcast([128, 128]),
+                ident_bf[:],
+            )
+        nc.scalar.activation(out=e_all[:, 0:1024], in_=eb[0][:], func=EXP)
+        nc.scalar.activation(out=e_all[:, 1024:1536], in_=eb[1][:], func=EXP)
+
+        perm, banks, grouped, codes, scales = {}, {}, {}, {}, {}
+
+        def permute(u, use_scalar, parts=1):
+            h, g = divmod(u, 2)
+            if u not in perm:
+                perm[u] = work.tile([128, 4, 2, 128], F32, name="perm", tag="perm", bufs=4, align_bytes=64)
+            words = raws[h][:].bitcast(F32)[:, :, 256 * g : 256 * g + 256].rearrange("q r (p u) -> q r u p", u=2)
+            w = 4 // parts
+            for i in range(parts):
+                rs = slice(i * w, (i + 1) * w)
+                if use_scalar:
+                    nc.scalar.copy(out=perm[u][:, rs], in_=words[:, rs])
+                else:
+                    nc.vector.tensor_copy(out=perm[u][:, rs], in_=words[:, rs])
+
+        def turn(u):
+            for b in range(2):
+                ps = psum.tile([128, 2, 256], F32, name="tp", tag="tp", bufs=4)
+                banks[u, b] = ps
+                for r in range(2):
+                    for w in range(2):
+                        nc.tensor.transpose(ps[:, w, 128 * r : 128 * r + 128], perm[u][:, 2 * b + r, w, :], ident[:])
+
+        def evac(u, b, use_scalar):
+            if u not in grouped:
+                grouped[u] = work.tile([128, N, 4], BF16, name="grouped", tag="grouped", bufs=4, align_bytes=64)
+            dst = grouped[u][:].bitcast(F32)[:, 256 * b : 256 * b + 256, :]
+            src = banks[u, b][:].rearrange("p u c -> p c u")
+            if use_scalar:
+                nc.scalar.copy(out=dst, in_=src)
+            else:
+                nc.vector.tensor_copy(out=dst, in_=src)
+
+        def quant(u):
+            codes[u] = work.tile([128, N], U32, name="codes", tag="codes", bufs=8, align_bytes=64)
+            scales[u] = work.tile([128, N], U8, name="scales", tag="scales", bufs=8, align_bytes=64)
+            nc.vector.quantize_mx(
+                out=codes[u][:].bitcast(E4X4), scales=scales[u][:], in_=grouped[u][:].rearrange("p c t -> p (c t)")
+            )
+
+        def mm(m, u):
+            g = u % 8
+            if g == 0:
+                acc[m] = new_acc(m, [128, N], F32)
+            nc.tensor.matmul_mx(
+                acc[m][:],
+                lhsT=gw[:, g, 128 * m : 128 * m + 128].bitcast(E5X4),
+                lhsT_scale=gs[:, g, 128 * m : 128 * m + 128],
+                rhs=codes[u][:].bitcast(E4X4),
+                rhs_scale=scales[u][:],
+                start=(g == 0),
+                stop=(g == 7),
+            )
+
+        outs = {}
+
+        def op1(s, m, cols=slice(0, N)):
+            if (s, m) not in outs:
+                outs[s, m] = work.tile([128, N], F32, name="o", tag="o", bufs=8, align_bytes=64)
+            nc.vector.scalar_tensor_tensor(
+                out=outs[s, m][:, cols],
+                in0=acc[m][:, cols],
+                scalar=neg_eta[:, m : m + 1],
+                in1=dirs[s][:, m, cols],
+                op0=MULT,
+                op1=ADD,
+            )
+
+        def op2(s, m, lo=0, hi=N):
+            o = outs[s, m]
+            nc.vector.tensor_tensor(out=o[:, lo:hi], in0=o[:, lo:hi], in1=e_all[:, s * N + lo : s * N + hi], op=MULT)
+
+        def store(s, m, lo=0, hi=N):
+            nc.sync.dma_start(
+                out=out[128 * m : 128 * m + 128, s * N + lo : s * N + hi], in_=outs[s, m][:, lo:hi]
+            )
+
+        permute(0, False, 2)
+        permute(1, False, 2)
+        turn(0)
+        turn(1)
+        evac(0, 0, False)
+        evac(0, 1, True)
+        quant(0)
+        evac(1, 0, False)
+        evac(1, 1, True)
+        quant(1)
+        permute(2, False)
+        permute(3, True)
+        for u in (0, 1):
+            for m in range(4):
+                mm(m, u)
+
+        for h in range(NP - 1):
+            a, b = 2 * h + 2, 2 * h + 3
+            turn(a)
+            turn(b)
+            for u in (a, b):
+                evac(u, 0, True)
+                evac(u, 1, True)
+            if h % 4 == 0 and h > 0:
+                op1(h // 4 - 1, 2)
+                op1(h // 4 - 1, 3)
+            quant(a)
+            if h + 2 < NP:
+                permute(a + 2, False)
+                permute(b + 2, True)
+            quant(b)
+            if h == NP - 2:
+                break
+            if h > 0:
+                for m in range(4):
+                    mm(m, 2 * h)
+                    mm(m, 2 * h + 1)
+            if h % 4 == 3:
+                op1(h // 4, 0)
+                op1(h // 4, 1)
+            if h % 4 == 0 and h > 0:
+                op2(h // 4 - 1, 0)
+                op2(h // 4 - 1, 1)
+            if h % 4 == 1 and h > 1:
+                s = h // 4 - 1
+                op2(s, 2)
+                op2(s, 3)
+                for m in range(4):
+                    store(s, m)
+                if s == 0:
+                    load_m(10, WHOLE)
+                    load_m(11, WHOLE)
+
+        for m, us in ((3, (20, 21)), (2, (20, 21)), (0, (20, 21, 22, 23)), (1, (20, 21, 22, 23)), (2, (22, 23)), (3, (22, 23))):
+            for u in us:
+                mm(m, u)
+        for m in range(4):
+            op1(2, m, slice(0, 256))
+            op1(2, m, slice(256, 512))
+            op2(2, m, 0, 256)
+            op2(2, m, 256, 512)
+            if m < 3:
+                store(2, m)
+            else:
+                store(2, m, 0, 256)
+                store(2, m, 256, 512)

@@ -3,24 +3,33 @@ from contextlib import ExitStack
 import concourse.mybir as mybir
 from concourse.masks import make_identity
 
-T, K, J = 512, 4096, 1536
-FLOPS = 2 * T * K * J
+TASKS, K, HYPER = 512, 4096, 1536
+FLOPS = 2 * TASKS * K * HYPER
 
 F32 = mybir.dt.float32
 BF16 = mybir.dt.bfloat16
 I32 = mybir.dt.int32
 U32 = mybir.dt.uint32
 U8 = mybir.dt.uint8
-E4X4 = mybir.dt.float8_e4m3fn_x4
-E5X4 = mybir.dt.float8_e5m2_x4
-EXP = mybir.ActivationFunctionType.Exp
+E4M3_X4 = mybir.dt.float8_e4m3fn_x4
+E5M2_X4 = mybir.dt.float8_e5m2_x4
 MULT = mybir.AluOpType.mult
 ADD = mybir.AluOpType.add
+EXP = mybir.ActivationFunctionType.Exp
 
-N = 512
-SWEEPS = J // N
-PAIRS = K // 1024
-NP = SWEEPS * PAIRS
+P = 128
+COLS = 512
+K_PASS = 512
+PASSES = K // K_PASS
+BLOCKS = HYPER // COLS
+UNITS = BLOCKS * PASSES
+TASK_TILES = TASKS // P
+ROW_TILES = COLS // P
+K_LOAD = 2 * K_PASS
+LOADS_PER_BLOCK = K // K_LOAD
+
+ROUNDS = (4, 4, 4) + 2 * (3, 3, 4, 3, 3)
+AHEAD = 3
 
 
 def tile_multitask_unrolled_hypergradient_e1_kernel(
@@ -29,231 +38,236 @@ def tile_multitask_unrolled_hypergradient_e1_kernel(
     nc = tc.nc
     with ExitStack() as ctx:
         keep = ctx.enter_context(tc.tile_pool(name="keep", bufs=1))
-        work = ctx.enter_context(tc.tile_pool(name="work", bufs=4))
+        work = ctx.enter_context(tc.tile_pool(name="work", bufs=8))
         psum = ctx.enter_context(tc.psum_pool(name="psum", bufs=1))
         ctx.enter_context(tc.manual_schedule())
 
-        gw = keep.tile([128, 8, T], U32, name="gw", align_bytes=64)
-        gs = keep.tile([128, 8, T], U8, name="gs", align_bytes=64)
-        vec = keep.tile([128, 128], BF16, name="vec", align_bytes=64)
-        vect = keep.tile([128, 16], BF16, name="vect", align_bytes=64)
-        neg_eta = keep.tile([128, 4], F32, name="neg_eta")
-        e_all = keep.tile([128, J], F32, name="e_all", align_bytes=64)
-        ident = keep.tile([128, 128], F32, name="ident", align_bytes=64)
-        ident_bf = keep.tile([128, 128], BF16, name="ident_bf", align_bytes=64)
+        g_codes = keep.tile([P, PASSES, TASKS], U32, name="g_codes", align_bytes=256)
+        g_plane = keep.tile([P, PASSES, TASKS], U8, name="g_plane", align_bytes=256)
+        vectors = keep.tile([P, P], BF16, name="vectors", align_bytes=256)
+        exp_rho = keep.tile([P, HYPER // P], F32, name="exp_rho", align_bytes=256)
+        neg_eta = keep.tile([P, TASK_TILES], F32, name="neg_eta", align_bytes=256)
+        exp_all = keep.tile([P, HYPER], F32, name="exp_all", align_bytes=256)
+        ident_f32 = keep.tile([P, P], F32, name="ident_f32", align_bytes=256)
+        ident_bf16 = keep.tile([P, P], BF16, name="ident_bf16", align_bytes=256)
 
-        raws = {}
-        dirs = {}
+        make_identity(nc, ident_f32[:])
+        make_identity(nc, ident_bf16[:])
+        nc.vector.memset(vectors[:], 0.0)
+        nc.vector.memset(g_plane[:].bitcast(I32), 0)
 
-        def load_m(h, pieces):
-            s, q = divmod(h, PAIRS)
-            raw = work.tile([128, 4, 1024], BF16, name="raw", tag="raw", bufs=12, align_bytes=64)
-            raws[h] = raw
-            src = mixed[s * N : (s + 1) * N, q * 1024 : (q + 1) * 1024].rearrange("(r p) k -> p r k", p=128)
-            for rs, ks in pieces:
-                nc.sync.dma_start(out=raw[:, rs, ks], in_=src[:, rs, ks])
+        raw = {}
+        direct_sb = {}
 
-        def load_g(q):
-            src = g_words.rearrange("g p n t -> g p (n t)").bitcast(I32)
-            nc.sync.dma_start(
-                out=gw[:, 2 * q : 2 * q + 2, :].bitcast(I32),
-                in_=src[2 * q : 2 * q + 2].rearrange("g p n -> p g n"),
-            )
+        def load_mixed(n, row_step=ROW_TILES, k_step=K_LOAD):
+            block, part = divmod(n, LOADS_PER_BLOCK)
+            raw[n] = work.tile([P, ROW_TILES, K_LOAD], BF16, name="raw", tag="raw", bufs=12, align_bytes=256)
+            src = mixed[block * COLS : (block + 1) * COLS, part * K_LOAD : (part + 1) * K_LOAD]
+            src = src.rearrange("(r p) k -> p r k", p=P)
+            for k0 in range(0, K_LOAD, k_step):
+                for r0 in range(0, ROW_TILES, row_step):
+                    piece = (slice(None), slice(r0, r0 + row_step), slice(k0, k0 + k_step))
+                    nc.sync.dma_start(out=raw[n][piece], in_=src[piece])
 
-        def load_d(s):
-            d = keep.tile([128, 4, N], BF16, name="d%d" % s, align_bytes=64)
-            dirs[s] = d
-            nc.sync.dma_start(out=d[:], in_=direct[:, s * N : (s + 1) * N].rearrange("(m p) j -> p m j", p=128))
+        def load_vectors():
+            rho_rows = rho.rearrange("(c p) -> c p", p=P)
+            nc.sync.dma_start(out=vectors[0:8, :], in_=rho_rows[0:8])
+            nc.sync.dma_start(out=vectors[8:12, :], in_=rho_rows[8:12])
+            nc.sync.dma_start(out=vectors[12:16, :], in_=eta.rearrange("(c p) -> c p", p=P))
 
-        WHOLE = [(slice(0, 4), slice(0, 1024))]
-        nc.vector.memset(vec[:], 0.0)
-        nc.scalar.dma_start(out=vec[0:12, :], in_=rho.rearrange("(c p) -> c p", p=128))
-        nc.scalar.dma_start(out=vec[12:16, :], in_=eta.rearrange("(c p) -> c p", p=128))
-        make_identity(nc, ident_bf[:])
-        make_identity(nc, ident[:])
-        nc.vector.memset(gs[:].bitcast(I32), 0)
-        load_m(0, [(slice(2 * b, 2 * b + 2), slice(512 * g, 512 * g + 512)) for g in range(2) for b in range(2)])
-        for Q in range(4):
-            nc.sync.dma_start(
-                out=gs[32 * Q : 32 * Q + 4].bitcast(I32),
-                in_=g_scales[:, 4 * Q : 4 * Q + 4, :].bitcast(I32).rearrange("g r n -> r g n"),
-            )
+        def load_g(n):
+            words = g_words.rearrange("g p n t -> g p (n t)").bitcast(I32)
+            two = slice(2 * n, 2 * n + 2)
+            nc.sync.dma_start(out=g_codes[:, two, :].bitcast(I32), in_=words[two].rearrange("g p n -> p g n"))
+
+        def load_scales(lo, hi):
+            for quadrant in range(4):
+                nc.sync.dma_start(
+                    out=g_plane[32 * quadrant : 32 * quadrant + 4, lo:hi].bitcast(I32),
+                    in_=g_scales[lo:hi, 4 * quadrant : 4 * quadrant + 4, :].bitcast(I32).rearrange("g r n -> r g n"),
+                )
+
+        def load_direct(block):
+            direct_sb[block] = keep.tile([P, TASK_TILES, COLS], BF16, name="direct%d" % block, align_bytes=256)
+            src = direct[:, block * COLS : (block + 1) * COLS].rearrange("(m p) j -> p m j", p=P)
+            nc.sync.dma_start(out=direct_sb[block][:], in_=src)
+
+        load_mixed(0, row_step=2, k_step=K_PASS)
+        load_vectors()
+        load_mixed(1)
         load_g(0)
-        load_m(1, WHOLE)
-        load_m(2, WHOLE)
+        load_scales(0, 2)
+        load_mixed(2)
         load_g(1)
-        load_m(3, WHOLE)
+        load_scales(2, 4)
+        load_mixed(3)
+        load_mixed(4)
+        load_scales(4, 8)
         load_g(2)
-        load_m(4, WHOLE)
         load_g(3)
-        load_d(0)
-        load_m(5, WHOLE)
-        load_m(6, WHOLE)
-        load_d(1)
-        load_m(7, WHOLE)
-        load_m(8, WHOLE)
-        load_m(9, WHOLE)
-        load_d(2)
+        load_mixed(5)
+        load_direct(0)
+        load_mixed(6)
+        load_direct(1)
+        load_mixed(7)
+        load_mixed(8)
+        load_mixed(9)
+        load_direct(2)
+        load_mixed(10)
+        load_mixed(11)
 
-        acc = {}
+        permuted, banks, grouped, codes, plane = {}, {}, {}, {}, {}
 
-        def new_acc(m, shape, dtype):
-            return psum.tile(shape, dtype, name="acc%d" % m, tag="acc%d" % m, bufs=1)
-
-        vps = new_acc(2, [128, 128], BF16)
-        nc.tensor.transpose(vps[:], vec[:], ident_bf[:])
-        nc.vector.tensor_copy(out=vect[:], in_=vps[:, 0:16])
-        nc.vector.tensor_scalar(out=neg_eta[:], in0=vect[:, 12:16], scalar1=-1.0, scalar2=None, op0=MULT)
-        eb = [new_acc(0, [128, 1024], BF16), new_acc(1, [128, 512], BF16)]
-        for c in range(12):
-            nc.tensor.transpose(
-                eb[c // 8][:, (c % 8) * 128 : (c % 8 + 1) * 128],
-                vect[:, c : c + 1].to_broadcast([128, 128]),
-                ident_bf[:],
-            )
-        nc.scalar.activation(out=e_all[:, 0:1024], in_=eb[0][:], func=EXP)
-        nc.scalar.activation(out=e_all[:, 1024:1536], in_=eb[1][:], func=EXP)
-
-        perm, banks, grouped, codes, scales = {}, {}, {}, {}, {}
-
-        def permute(u, use_scalar, parts=1):
-            h, g = divmod(u, 2)
-            if u not in perm:
-                perm[u] = work.tile([128, 4, 2, 128], F32, name="perm", tag="perm", bufs=4, align_bytes=64)
-            words = raws[h][:].bitcast(F32)[:, :, 256 * g : 256 * g + 256].rearrange("q r (p u) -> q r u p", u=2)
-            w = 4 // parts
-            for i in range(parts):
-                rs = slice(i * w, (i + 1) * w)
-                if use_scalar:
-                    nc.scalar.copy(out=perm[u][:, rs], in_=words[:, rs])
+        def permute(u, pieces=1):
+            n, g = divmod(u, 2)
+            permuted[u] = work.tile([P, ROW_TILES, 2, P], F32, name="permuted", tag="permuted", bufs=6, align_bytes=256)
+            words = raw[n][:].bitcast(F32)[:, :, 2 * P * g : 2 * P * (g + 1)].rearrange("q r (p w) -> q r w p", w=2)
+            step = ROW_TILES // pieces
+            for r0 in range(0, ROW_TILES, step):
+                rows = slice(r0, r0 + step)
+                if u % 4 == 3:
+                    nc.scalar.copy(out=permuted[u][:, rows], in_=words[:, rows])
                 else:
-                    nc.vector.tensor_copy(out=perm[u][:, rs], in_=words[:, rs])
+                    nc.vector.tensor_copy(out=permuted[u][:, rows], in_=words[:, rows])
 
-        def turn(u):
-            for b in range(2):
-                ps = psum.tile([128, 2, 256], F32, name="tp", tag="tp", bufs=4)
-                banks[u, b] = ps
-                for r in range(2):
-                    for w in range(2):
-                        nc.tensor.transpose(ps[:, w, 128 * r : 128 * r + 128], perm[u][:, 2 * b + r, w, :], ident[:])
+        def turn(u, half):
+            bank = psum.tile([P, 2, 2 * P], F32, name="bank", tag="bank", bufs=4)
+            for r in range(2):
+                for w in range(2):
+                    nc.tensor.transpose(bank[:, w, P * r : P * (r + 1)], permuted[u][:, 2 * half + r, w, :], ident_f32[:])
+            banks[u, half] = bank
 
-        def evac(u, b, use_scalar):
-            if u not in grouped:
-                grouped[u] = work.tile([128, N, 4], BF16, name="grouped", tag="grouped", bufs=4, align_bytes=64)
-            dst = grouped[u][:].bitcast(F32)[:, 256 * b : 256 * b + 256, :]
-            src = banks[u, b][:].rearrange("p u c -> p c u")
-            if use_scalar:
+        def empty(u, half, on_scalar=True):
+            if half == 0:
+                grouped[u] = work.tile([P, COLS, 4], BF16, name="grouped", tag="grouped", bufs=5, align_bytes=256)
+            dst = grouped[u][:].bitcast(F32)[:, 2 * P * half : 2 * P * (half + 1), :]
+            src = banks[u, half][:].rearrange("p w c -> p c w")
+            if on_scalar:
                 nc.scalar.copy(out=dst, in_=src)
             else:
                 nc.vector.tensor_copy(out=dst, in_=src)
 
-        def quant(u):
-            codes[u] = work.tile([128, N], U32, name="codes", tag="codes", bufs=8, align_bytes=64)
-            scales[u] = work.tile([128, N], U8, name="scales", tag="scales", bufs=8, align_bytes=64)
+        def quantise(u):
+            codes[u] = work.tile([P, COLS], U32, name="codes", tag="codes", bufs=8, align_bytes=256)
+            plane[u] = work.tile([P, COLS], U8, name="plane", tag="plane", bufs=8, align_bytes=256)
             nc.vector.quantize_mx(
-                out=codes[u][:].bitcast(E4X4), scales=scales[u][:], in_=grouped[u][:].rearrange("p c t -> p (c t)")
+                out=codes[u][:].bitcast(E4M3_X4),
+                scales=plane[u][:],
+                in_=grouped[u][:].rearrange("p c t -> p (c t)"),
             )
 
-        def mm(m, u):
-            g = u % 8
+        sums, result = {}, {}
+
+        def sum_bank(m, shape, dtype):
+            return psum.tile(shape, dtype, name="sum%d" % m, tag="sum%d" % m, bufs=1)
+
+        def multiply(u, m):
+            g = u % PASSES
+            tasks = slice(P * m, P * (m + 1))
             if g == 0:
-                acc[m] = new_acc(m, [128, N], F32)
+                sums[m] = sum_bank(m, [P, COLS], F32)
             nc.tensor.matmul_mx(
-                acc[m][:],
-                lhsT=gw[:, g, 128 * m : 128 * m + 128].bitcast(E5X4),
-                lhsT_scale=gs[:, g, 128 * m : 128 * m + 128],
-                rhs=codes[u][:].bitcast(E4X4),
-                rhs_scale=scales[u][:],
+                sums[m][:],
+                lhsT=g_codes[:, g, tasks].bitcast(E5M2_X4),
+                lhsT_scale=g_plane[:, g, tasks],
+                rhs=codes[u][:].bitcast(E4M3_X4),
+                rhs_scale=plane[u][:],
                 start=(g == 0),
-                stop=(g == 7),
+                stop=(g == PASSES - 1),
             )
 
-        outs = {}
-
-        def op1(s, m, cols=slice(0, N)):
-            if (s, m) not in outs:
-                outs[s, m] = work.tile([128, N], F32, name="o", tag="o", bufs=8, align_bytes=64)
+        def add_direct(block, m, lo, hi):
+            if lo == 0:
+                result[block, m] = work.tile([P, COLS], F32, name="result", tag="result", bufs=8, align_bytes=256)
             nc.vector.scalar_tensor_tensor(
-                out=outs[s, m][:, cols],
-                in0=acc[m][:, cols],
+                out=result[block, m][:, lo:hi],
+                in0=sums[m][:, lo:hi],
                 scalar=neg_eta[:, m : m + 1],
-                in1=dirs[s][:, m, cols],
+                in1=direct_sb[block][:, m, lo:hi],
                 op0=MULT,
                 op1=ADD,
             )
 
-        def op2(s, m, lo=0, hi=N):
-            o = outs[s, m]
-            nc.vector.tensor_tensor(out=o[:, lo:hi], in0=o[:, lo:hi], in1=e_all[:, s * N + lo : s * N + hi], op=MULT)
+        def times_exp(block, m, lo, hi):
+            part = result[block, m][:, lo:hi]
+            nc.vector.tensor_tensor(out=part, in0=part, in1=exp_all[:, block * COLS + lo : block * COLS + hi], op=MULT)
 
-        def store(s, m, lo=0, hi=N):
-            nc.sync.dma_start(
-                out=out[128 * m : 128 * m + 128, s * N + lo : s * N + hi], in_=outs[s, m][:, lo:hi]
-            )
+        def store(block, m, lo, hi):
+            dst = out[P * m : P * (m + 1), block * COLS + lo : block * COLS + hi]
+            nc.sync.dma_start(out=dst, in_=result[block, m][:, lo:hi])
 
-        permute(0, False, 2)
-        permute(1, False, 2)
-        turn(0)
-        turn(1)
-        evac(0, 0, False)
-        evac(0, 1, True)
-        quant(0)
-        evac(1, 0, False)
-        evac(1, 1, True)
-        quant(1)
-        permute(2, False)
-        permute(3, True)
+        def spread_exp(block):
+            bank = psum.tile([P, ROW_TILES, P], F32, name="bank", tag="bank", bufs=4)
+            for r in range(ROW_TILES):
+                c = ROW_TILES * block + r
+                nc.tensor.transpose(bank[:, r, :], exp_rho[:, c : c + 1].to_broadcast([P, P]), ident_f32[:])
+            dst = exp_all[:, block * COLS : (block + 1) * COLS]
+            nc.scalar.copy(out=dst.rearrange("p (r c) -> p r c", r=ROW_TILES), in_=bank[:])
+
         for u in (0, 1):
-            for m in range(4):
-                mm(m, u)
+            permute(u, pieces=2)
+        for u in (0, 1):
+            for half in (0, 1):
+                turn(u, half)
+        vectors_t = sum_bank(2, [P, P], BF16)
+        nc.tensor.transpose(vectors_t[:], vectors[:], ident_bf16[:])
+        for u in (0, 1):
+            empty(u, 0, on_scalar=False)
+            empty(u, 1)
+            quantise(u)
+        nc.vector.tensor_scalar(out=neg_eta[:], in0=vectors_t[:, 12:16], scalar1=-1.0, scalar2=None, op0=MULT)
+        nc.scalar.activation(out=exp_rho[:], in_=vectors_t[:, 0:12], func=EXP)
+        for block in range(BLOCKS):
+            spread_exp(block)
+        for m in range(TASK_TILES):
+            multiply(0, m)
+        for u in range(2, 2 + AHEAD):
+            permute(u)
 
-        for h in range(NP - 1):
-            a, b = 2 * h + 2, 2 * h + 3
-            turn(a)
-            turn(b)
-            for u in (a, b):
-                evac(u, 0, True)
-                evac(u, 1, True)
-            if h % 4 == 0 and h > 0:
-                op1(h // 4 - 1, 2)
-                op1(h // 4 - 1, 3)
-            quant(a)
-            if h + 2 < NP:
-                permute(a + 2, False)
-                permute(b + 2, True)
-            quant(b)
-            if h == NP - 2:
-                break
-            if h > 0:
-                for m in range(4):
-                    mm(m, 2 * h)
-                    mm(m, 2 * h + 1)
-            if h % 4 == 3:
-                op1(h // 4, 0)
-                op1(h // 4, 1)
-            if h % 4 == 0 and h > 0:
-                op2(h // 4 - 1, 0)
-                op2(h // 4 - 1, 1)
-            if h % 4 == 1 and h > 1:
-                s = h // 4 - 1
-                op2(s, 2)
-                op2(s, 3)
-                for m in range(4):
-                    store(s, m)
-                if s == 0:
-                    load_m(10, WHOLE)
-                    load_m(11, WHOLE)
+        order = [(u, m) for u in range(18) for m in range(TASK_TILES)]
+        order += [(u, m) for m in range(TASK_TILES) for u in range(18, 20)]
+        order += [(u, m) for m in range(TASK_TILES) for u in range(20, UNITS)]
+        order = order[TASK_TILES:]
+        halves = [(u, half) for u in range(2, UNITS) for half in range(2)]
+        unfinished = []
 
-        for m, us in ((3, (20, 21)), (2, (20, 21)), (0, (20, 21, 22, 23)), (1, (20, 21, 22, 23)), (2, (22, 23)), (3, (22, 23))):
-            for u in us:
-                mm(m, u)
-        for m in range(4):
-            op1(2, m, slice(0, 256))
-            op1(2, m, slice(256, 512))
-            op2(2, m, 0, 256)
-            op2(2, m, 256, 512)
-            if m < 3:
-                store(2, m)
-            else:
-                store(2, m, 0, 256)
-                store(2, m, 256, 512)
+        def run_passes(units, limit):
+            for _ in range(limit):
+                if not order or order[0][0] >= units:
+                    return
+                u, m = order.pop(0)
+                multiply(u, m)
+                block = u // PASSES
+                if u % PASSES < PASSES - 1:
+                    continue
+                if block < BLOCKS - 1:
+                    add_direct(block, m, 0, COLS)
+                    unfinished.append((block, m))
+                    continue
+                parts = [(0, COLS // 2), (COLS // 2, COLS)]
+                for lo, hi in parts:
+                    add_direct(block, m, lo, hi)
+                for lo, hi in parts:
+                    times_exp(block, m, lo, hi)
+                    if m == TASK_TILES - 1:
+                        store(block, m, lo, hi)
+                if m < TASK_TILES - 1:
+                    store(block, m, 0, COLS)
+
+        for i, run in enumerate(ROUNDS):
+            ready = halves[0][0]
+            for u, half in halves[:run]:
+                turn(u, half)
+                empty(u, half)
+                if half == 0:
+                    continue
+                if u + AHEAD < UNITS:
+                    permute(u + AHEAD)
+                quantise(u)
+                if unfinished:
+                    block, m = unfinished.pop(0)
+                    times_exp(block, m, 0, COLS)
+                    store(block, m, 0, COLS)
+            halves = halves[run:]
+            run_passes(ready, TASK_TILES if i == len(ROUNDS) - 2 else len(order))
+        run_passes(UNITS, len(order))

from contextlib import ExitStack

import concourse.mybir as mybir
from concourse.masks import make_identity

TASKS, K, HYPER = 512, 4096, 1536
FLOPS = 2 * TASKS * K * HYPER

F32 = mybir.dt.float32
BF16 = mybir.dt.bfloat16
I32 = mybir.dt.int32
U32 = mybir.dt.uint32
U8 = mybir.dt.uint8
E4M3_X4 = mybir.dt.float8_e4m3fn_x4
E5M2_X4 = mybir.dt.float8_e5m2_x4
MULT = mybir.AluOpType.mult
ADD = mybir.AluOpType.add
EXP = mybir.ActivationFunctionType.Exp

P = 128
COLS = 512
K_PASS = 512
PASSES = K // K_PASS
BLOCKS = HYPER // COLS
UNITS = BLOCKS * PASSES
TASK_TILES = TASKS // P
ROW_TILES = COLS // P
K_LOAD = 2 * K_PASS
LOADS_PER_BLOCK = K // K_LOAD

ROUNDS = (4, 4, 4) + 2 * (3, 3, 4, 3, 3)
AHEAD = 3


def tile_multitask_unrolled_hypergradient_e1_kernel(
    tc, g_words, g_scales, mixed, direct, eta, rho, out
):
    nc = tc.nc
    with ExitStack() as ctx:
        keep = ctx.enter_context(tc.tile_pool(name="keep", bufs=1))
        work = ctx.enter_context(tc.tile_pool(name="work", bufs=8))
        psum = ctx.enter_context(tc.psum_pool(name="psum", bufs=1))
        ctx.enter_context(tc.manual_schedule())

        g_codes = keep.tile([P, PASSES, TASKS], U32, name="g_codes", align_bytes=256)
        g_plane = keep.tile([P, PASSES, TASKS], U8, name="g_plane", align_bytes=256)
        vectors = keep.tile([P, P], BF16, name="vectors", align_bytes=256)
        exp_rho = keep.tile([P, HYPER // P], F32, name="exp_rho", align_bytes=256)
        neg_eta = keep.tile([P, TASK_TILES], F32, name="neg_eta", align_bytes=256)
        exp_all = keep.tile([P, HYPER], F32, name="exp_all", align_bytes=256)
        ident_f32 = keep.tile([P, P], F32, name="ident_f32", align_bytes=256)
        ident_bf16 = keep.tile([P, P], BF16, name="ident_bf16", align_bytes=256)

        make_identity(nc, ident_f32[:])
        make_identity(nc, ident_bf16[:])
        nc.vector.memset(vectors[:], 0.0)
        nc.vector.memset(g_plane[:].bitcast(I32), 0)

        raw = {}
        direct_sb = {}

        def load_mixed(n, row_step=ROW_TILES, k_step=K_LOAD):
            block, part = divmod(n, LOADS_PER_BLOCK)
            raw[n] = work.tile([P, ROW_TILES, K_LOAD], BF16, name="raw", tag="raw", bufs=12, align_bytes=256)
            src = mixed[block * COLS : (block + 1) * COLS, part * K_LOAD : (part + 1) * K_LOAD]
            src = src.rearrange("(r p) k -> p r k", p=P)
            for k0 in range(0, K_LOAD, k_step):
                for r0 in range(0, ROW_TILES, row_step):
                    piece = (slice(None), slice(r0, r0 + row_step), slice(k0, k0 + k_step))
                    nc.sync.dma_start(out=raw[n][piece], in_=src[piece])

        def load_vectors():
            rho_rows = rho.rearrange("(c p) -> c p", p=P)
            nc.sync.dma_start(out=vectors[0:8, :], in_=rho_rows[0:8])
            nc.sync.dma_start(out=vectors[8:12, :], in_=rho_rows[8:12])
            nc.sync.dma_start(out=vectors[12:16, :], in_=eta.rearrange("(c p) -> c p", p=P))

        def load_g(n):
            words = g_words.rearrange("g p n t -> g p (n t)").bitcast(I32)
            two = slice(2 * n, 2 * n + 2)
            nc.sync.dma_start(out=g_codes[:, two, :].bitcast(I32), in_=words[two].rearrange("g p n -> p g n"))

        def load_scales(lo, hi):
            for quadrant in range(4):
                nc.sync.dma_start(
                    out=g_plane[32 * quadrant : 32 * quadrant + 4, lo:hi].bitcast(I32),
                    in_=g_scales[lo:hi, 4 * quadrant : 4 * quadrant + 4, :].bitcast(I32).rearrange("g r n -> r g n"),
                )

        def load_direct(block):
            direct_sb[block] = keep.tile([P, TASK_TILES, COLS], BF16, name="direct%d" % block, align_bytes=256)
            src = direct[:, block * COLS : (block + 1) * COLS].rearrange("(m p) j -> p m j", p=P)
            nc.sync.dma_start(out=direct_sb[block][:], in_=src)

        load_mixed(0, row_step=2, k_step=K_PASS)
        load_vectors()
        load_mixed(1)
        load_g(0)
        load_scales(0, 2)
        load_mixed(2)
        load_g(1)
        load_scales(2, 4)
        load_mixed(3)
        load_mixed(4)
        load_scales(4, 8)
        load_g(2)
        load_g(3)
        load_mixed(5)
        load_direct(0)
        load_mixed(6)
        load_direct(1)
        load_mixed(7)
        load_mixed(8)
        load_mixed(9)
        load_direct(2)
        load_mixed(10)
        load_mixed(11)

        permuted, banks, grouped, codes, plane = {}, {}, {}, {}, {}

        def permute(u, pieces=1):
            n, g = divmod(u, 2)
            permuted[u] = work.tile([P, ROW_TILES, 2, P], F32, name="permuted", tag="permuted", bufs=6, align_bytes=256)
            words = raw[n][:].bitcast(F32)[:, :, 2 * P * g : 2 * P * (g + 1)].rearrange("q r (p w) -> q r w p", w=2)
            step = ROW_TILES // pieces
            for r0 in range(0, ROW_TILES, step):
                rows = slice(r0, r0 + step)
                if u % 4 == 3:
                    nc.scalar.copy(out=permuted[u][:, rows], in_=words[:, rows])
                else:
                    nc.vector.tensor_copy(out=permuted[u][:, rows], in_=words[:, rows])

        def turn(u, half):
            bank = psum.tile([P, 2, 2 * P], F32, name="bank", tag="bank", bufs=4)
            for r in range(2):
                for w in range(2):
                    nc.tensor.transpose(bank[:, w, P * r : P * (r + 1)], permuted[u][:, 2 * half + r, w, :], ident_f32[:])
            banks[u, half] = bank

        def empty(u, half, on_scalar=True):
            if half == 0:
                grouped[u] = work.tile([P, COLS, 4], BF16, name="grouped", tag="grouped", bufs=5, align_bytes=256)
            dst = grouped[u][:].bitcast(F32)[:, 2 * P * half : 2 * P * (half + 1), :]
            src = banks[u, half][:].rearrange("p w c -> p c w")
            if on_scalar:
                nc.scalar.copy(out=dst, in_=src)
            else:
                nc.vector.tensor_copy(out=dst, in_=src)

        def quantise(u):
            codes[u] = work.tile([P, COLS], U32, name="codes", tag="codes", bufs=8, align_bytes=256)
            plane[u] = work.tile([P, COLS], U8, name="plane", tag="plane", bufs=8, align_bytes=256)
            nc.vector.quantize_mx(
                out=codes[u][:].bitcast(E4M3_X4),
                scales=plane[u][:],
                in_=grouped[u][:].rearrange("p c t -> p (c t)"),
            )

        sums, result = {}, {}

        def sum_bank(m, shape, dtype):
            return psum.tile(shape, dtype, name="sum%d" % m, tag="sum%d" % m, bufs=1)

        def multiply(u, m):
            g = u % PASSES
            tasks = slice(P * m, P * (m + 1))
            if g == 0:
                sums[m] = sum_bank(m, [P, COLS], F32)
            nc.tensor.matmul_mx(
                sums[m][:],
                lhsT=g_codes[:, g, tasks].bitcast(E5M2_X4),
                lhsT_scale=g_plane[:, g, tasks],
                rhs=codes[u][:].bitcast(E4M3_X4),
                rhs_scale=plane[u][:],
                start=(g == 0),
                stop=(g == PASSES - 1),
            )

        def add_direct(block, m, lo, hi):
            if lo == 0:
                result[block, m] = work.tile([P, COLS], F32, name="result", tag="result", bufs=8, align_bytes=256)
            nc.vector.scalar_tensor_tensor(
                out=result[block, m][:, lo:hi],
                in0=sums[m][:, lo:hi],
                scalar=neg_eta[:, m : m + 1],
                in1=direct_sb[block][:, m, lo:hi],
                op0=MULT,
                op1=ADD,
            )

        def times_exp(block, m, lo, hi):
            part = result[block, m][:, lo:hi]
            nc.vector.tensor_tensor(out=part, in0=part, in1=exp_all[:, block * COLS + lo : block * COLS + hi], op=MULT)

        def store(block, m, lo, hi):
            dst = out[P * m : P * (m + 1), block * COLS + lo : block * COLS + hi]
            nc.sync.dma_start(out=dst, in_=result[block, m][:, lo:hi])

        def spread_exp(block):
            bank = psum.tile([P, ROW_TILES, P], F32, name="bank", tag="bank", bufs=4)
            for r in range(ROW_TILES):
                c = ROW_TILES * block + r
                nc.tensor.transpose(bank[:, r, :], exp_rho[:, c : c + 1].to_broadcast([P, P]), ident_f32[:])
            dst = exp_all[:, block * COLS : (block + 1) * COLS]
            nc.scalar.copy(out=dst.rearrange("p (r c) -> p r c", r=ROW_TILES), in_=bank[:])

        for u in (0, 1):
            permute(u, pieces=2)
        for u in (0, 1):
            for half in (0, 1):
                turn(u, half)
        vectors_t = sum_bank(2, [P, P], BF16)
        nc.tensor.transpose(vectors_t[:], vectors[:], ident_bf16[:])
        for u in (0, 1):
            empty(u, 0, on_scalar=False)
            empty(u, 1)
            quantise(u)
        nc.vector.tensor_scalar(out=neg_eta[:], in0=vectors_t[:, 12:16], scalar1=-1.0, scalar2=None, op0=MULT)
        nc.scalar.activation(out=exp_rho[:], in_=vectors_t[:, 0:12], func=EXP)
        for block in range(BLOCKS):
            spread_exp(block)
        for m in range(TASK_TILES):
            multiply(0, m)
        for u in range(2, 2 + AHEAD):
            permute(u)

        order = [(u, m) for u in range(18) for m in range(TASK_TILES)]
        order += [(u, m) for m in range(TASK_TILES) for u in range(18, 20)]
        order += [(u, m) for m in range(TASK_TILES) for u in range(20, UNITS)]
        order = order[TASK_TILES:]
        halves = [(u, half) for u in range(2, UNITS) for half in range(2)]
        unfinished = []

        def run_passes(units, limit):
            for _ in range(limit):
                if not order or order[0][0] >= units:
                    return
                u, m = order.pop(0)
                multiply(u, m)
                block = u // PASSES
                if u % PASSES < PASSES - 1:
                    continue
                if block < BLOCKS - 1:
                    add_direct(block, m, 0, COLS)
                    unfinished.append((block, m))
                    continue
                parts = [(0, COLS // 2), (COLS // 2, COLS)]
                for lo, hi in parts:
                    add_direct(block, m, lo, hi)
                for lo, hi in parts:
                    times_exp(block, m, lo, hi)
                    if m == TASK_TILES - 1:
                        store(block, m, lo, hi)
                if m < TASK_TILES - 1:
                    store(block, m, 0, COLS)

        for i, run in enumerate(ROUNDS):
            ready = halves[0][0]
            for u, half in halves[:run]:
                turn(u, half)
                empty(u, half)
                if half == 0:
                    continue
                if u + AHEAD < UNITS:
                    permute(u + AHEAD)
                quantise(u)
                if unfinished:
                    block, m = unfinished.pop(0)
                    times_exp(block, m, 0, COLS)
                    store(block, m, 0, COLS)
            halves = halves[run:]
            run_passes(ready, TASK_TILES if i == len(ROUNDS) - 2 else len(order))
        run_passes(UNITS, len(order))
